import numpy as np
import ml_dtypes


def mxq(x, axis, fmt="e4m3"):
    dtype, down = {"e4m3": (ml_dtypes.float8_e4m3fn, 7), "e5m2": (ml_dtypes.float8_e5m2, 14)}[fmt]
    v = np.moveaxis(np.asarray(x, np.float32).astype(ml_dtypes.bfloat16).astype(np.float64), axis, -1)
    blocks = v.reshape(v.shape[:-1] + (-1, 32))
    amax = np.abs(blocks).max(-1, keepdims=True)
    byte = np.maximum(np.where(amax > 0, np.frexp(amax)[1] - 1 + 127, 0) - down, 1)
    scale = np.exp2(byte - 127.0)
    codes = (blocks / scale).astype(np.float32).astype(dtype).astype(np.float64)
    return np.moveaxis((codes * scale).reshape(v.shape), -1, axis)


WIDE = False


def mx_kscale(k):
    if not WIDE:
        return np.ones(k)
    levels = np.array([10, -10, 5, -5, 0])
    if k % 512:
        return np.exp2(np.random.permutation(np.resize(levels, k // 32))).repeat(32)
    a = np.empty((k // 512, 16))
    for p in range(k // 512):
        a[p, :8] = np.random.permutation(np.resize(levels, 8))
        for g in range(8):
            far = levels[np.abs(levels - a[p, g]) >= 10]
            a[p, g + 8] = far[np.random.randint(len(far))]
    return np.exp2(a.ravel()).repeat(32)


def f64(x):
    return np.asarray(x).astype(np.float64)


def striped(idx):
    return np.tile(idx.reshape(-1, 16).T, (8, 1)).astype(np.uint16)


def unstriped(offs):
    return offs[:16].T.reshape(-1).astype(np.int64)


def striped8(idx):
    return np.concatenate([x.reshape(-1, 16).T for x in idx]).astype(np.uint16)


def runs(offs, k):
    lists = np.stack([offs[16 * r : 16 * r + 16].T.reshape(-1) for r in range(8)]).astype(np.int64)
    return lists[np.arange(k) % 512 // 64]


def pack_weight(w):
    k, n = w.shape
    w = f64(np.asarray(w, np.float32).astype(ml_dtypes.bfloat16)).reshape(k // 32, 32, n)
    amax = np.abs(w).max(1)
    byte = np.clip(np.where(amax > 0, np.frexp(amax)[1] - 1 + 127 - 7, 1), 1, 254)
    scaled = (w * np.exp2(127.0 - byte)[:, None, :]).reshape(k, n).astype(np.float32)
    words = np.ascontiguousarray(scaled.reshape(k // 512, 128, 4, n).transpose(0, 1, 3, 2)).astype(ml_dtypes.float8_e4m3fn).view(np.uint8)
    return words, np.ascontiguousarray(byte.astype(np.uint8).reshape(k // 512, 16, n))


def unpack_weight(words, scales):
    g, p, n, _ = words.shape
    vals = np.ascontiguousarray(words).view(ml_dtypes.float8_e4m3fn).astype(np.float64) * np.repeat(np.exp2(scales.astype(np.float64) - 127.0), 8, axis=1)[..., None]
    return vals.transpose(0, 1, 3, 2).reshape(g * 512, n)


def sigmoid(v):
    return 1.0 / (1.0 + np.exp(-np.maximum(v, -700.0)))


K, T, S, N, G, H, W = 512, 2048, 512, 512, 2048, 512, 256


def setup_inputs():
    n = np.random.standard_normal
    s = mx_kscale(K)[:, None]
    u = mx_kscale(S)
    packed_xT = pack_weight(n((K, T)) * s)
    packed_dT = pack_weight(n((K, G)) / s)
    perm = np.random.permutation(S)
    return {
        "x_words": packed_xT[0],
        "x_scales": packed_xT[1],
        "d_words": packed_dT[0],
        "d_scales": packed_dT[1],
        "gn": (np.random.uniform(0.5, 1.5, (H, 1)) * u[:, None]).astype(np.float32),
        "w1": (n((H, N)) / np.sqrt(H) / u[:, None]).astype(np.float32),
        "offs": striped(np.random.permutation(T)[:S]),
        "k1": striped8(np.random.randint(0, G, (8, H))),
        "n1": striped(perm[:W]),
        "n2": striped(perm[W:]),
        "n3": striped(np.random.randint(0, S, G)),
    }


def reference(x_words, x_scales, d_words, d_scales, gn, w1, offs, k1, n1, n2, n3):
    d_k1 = unpack_weight(d_words, d_scales)[np.arange(K)[:, None], runs(k1, K)]
    xq = unpack_weight(x_words, x_scales)[:, unstriped(offs)]
    h = 0.0625 * (d_k1.T @ xq)
    pa = h[:, unstriped(n1)]
    pb = h[:, unstriped(n2)]
    ra = pa * sigmoid(pb)
    ds = h.copy()
    ds[:, unstriped(n2)] = ra
    z = f64(gn) * ds
    h2 = mxq(f64(w1), 0, "e4m3").T @ mxq(z, 0, "e4m3")
    mb = h2[:, unstriped(n3)]
    mx = mb.reshape(N, S, 4).max(axis=2)
    mn = mb.reshape(N, S, 4).min(axis=2)
    return mx * np.tanh(h2 - mn)

@@ -1,0 +1,243 @@
+from contextlib import ExitStack
+
+import concourse.mybir as mybir
+
+K, T, S, N, G, H, W = 512, 2048, 512, 512, 2048, 512, 256
+FLOPS = 2 * K * H * S + 2 * H * N * S
+
+F32 = mybir.dt.float32
+BF16 = mybir.dt.bfloat16
+I32 = mybir.dt.int32
+U32 = mybir.dt.uint32
+U16 = mybir.dt.uint16
+U8 = mybir.dt.uint8
+FP8X4 = mybir.dt.float8_e4m3fn_x4
+ALU = mybir.AluOpType
+ACT = mybir.ActivationFunctionType
+
+P = 128
+PACK = 4
+HALF = S // 2
+PIECE = 512
+SPARE = 16
+H_SCALE = 0.0625
+
+
+def tile_picked_pqlayfoldgtan_none_p_kernel(
+    tc, x_words, x_scales, d_words, d_scales, gn, w1, offs, k1, n1, n2, n3, out
+):
+    nc = tc.nc
+    with ExitStack() as ctx:
+        lists = ctx.enter_context(tc.tile_pool(name="lists", bufs=1))
+        keep = ctx.enter_context(tc.tile_pool(name="keep", bufs=1))
+        ring = ctx.enter_context(tc.tile_pool(name="ring", bufs=3))
+        psum = ctx.enter_context(tc.psum_pool(name="psum", bufs=1))
+
+        def load_list(src, name):
+            tile = lists.tile([P, src.shape[1]], U16, name=name)
+            nc.sync.dma_start(tile[:], src)
+            return tile
+
+        def load_words(src, name):
+            tile = keep.tile([P, src.shape[2]], U32, name=name, align_bytes=64)
+            nc.sync.dma_start(tile[:].bitcast(I32), src[0].rearrange("p n t -> p (n t)").bitcast(I32))
+            return tile
+
+        k1_t = load_list(k1, "k1_t")
+        d_rows = keep.tile([P, G], U8, name="d_rows", align_bytes=64)
+        nc.sync.dma_start(
+            d_rows[:].bitcast(I32), d_scales[0].bitcast(I32).unsqueeze(1).broadcast_to([16, 8, G // 4])
+        )
+        offs_t = load_list(offs, "offs_t")
+        d_table = load_words(d_words, "d_table")
+        x_rows = keep.tile([P, T], U8, name="x_rows", align_bytes=64)
+        nc.vector.memset(x_rows[:].bitcast(I32), 0)
+        for q in range(4):
+            nc.scalar.dma_start(x_rows[32 * q : 32 * q + 4, :].bitcast(I32), x_scales[0, 4 * q : 4 * (q + 1), :].bitcast(I32))
+        x_table = load_words(x_words, "x_table")
+        n2_t = load_list(n2, "n2_t")
+        n1_t = load_list(n1, "n1_t")
+        n3_t = load_list(n3, "n3_t")
+
+        d_plane = keep.tile([P, H], U8, name="d_plane", align_bytes=64)
+        nc.vector.memset(d_plane[:].bitcast(I32), 0)
+        h2 = [keep.tile([P, S + SPARE], F32, name=f"h2_{m}") for m in range(N // P)]
+        for m in range(N // P):
+            nc.vector.memset(h2[m][:, S:], 0.0)
+
+        d_bytes = keep.tile([P, H], U8, name="d_bytes", align_bytes=64)
+        nc.vector.tensor_copy(d_bytes[:], d_rows[:].indirect(k1_t[:]))
+        d_dealt = keep.tile([P, H], U8, name="d_dealt", tag="w_raw", align_bytes=64)
+        nc.vector.tensor_copy(
+            d_dealt[:].rearrange("p (t m) -> p m t", t=PACK), d_bytes[:].rearrange("p (m t) -> p m t", t=PACK)
+        )
+        for q in range(4):
+            nc.scalar.dma_start(
+                d_plane[32 * q : 32 * q + 4, :].bitcast(I32), d_dealt[32 * q : 32 * (q + 1) : 8, :].bitcast(I32)
+            )
+
+        w_raw = keep.tile([P, PACK, N], F32, name="w_raw", tag="w_raw", align_bytes=64)
+        nc.sync.dma_start(w_raw[:], w1.rearrange("(p j) n -> p j n", j=PACK))
+
+        d_picked = keep.tile([P, H], U32, name="d_picked", tag="gain", align_bytes=64)
+        nc.vector.tensor_copy(d_picked[:], d_table[:].indirect(k1_t[:]))
+        d_codes = keep.tile([P, H], U32, name="d_codes", align_bytes=64)
+        nc.vector.tensor_copy(
+            d_codes[:].bitcast(I32).rearrange("p (t m) -> p m t", t=PACK),
+            d_picked[:].bitcast(I32).rearrange("p (m t) -> p m t", t=PACK),
+        )
+        x_plane = keep.tile([P, S], U8, name="x_plane", align_bytes=64)
+        nc.vector.tensor_copy(x_plane[:], x_rows[:].indirect(offs_t[:]))
+        gain = keep.tile([P, PACK], F32, name="gain", tag="gain", align_bytes=64)
+        nc.sync.dma_start(gain[:], gn.rearrange("(p t) o -> p (t o)", t=PACK))
+        x_codes = [keep.tile([P, HALF], U32, name=f"x_codes{u}", align_bytes=64) for u in range(2)]
+        for u in range(2):
+            nc.vector.tensor_copy(x_codes[u][:], x_table[:].indirect(offs_t[:, u * HALF // 16 : (u + 1) * HALF // 16]))
+        h_acc = {}
+        for t in range(PACK):
+            for u in range(2):
+                h_acc[t, u] = psum.tile([P, HALF], F32, name=f"h_acc{t}{u}", tag=f"bank{2 * t + u}")
+                nc.tensor.matmul_mx(
+                    out=h_acc[t, u][:],
+                    lhsT=d_codes[:, t * P : (t + 1) * P].bitcast(FP8X4),
+                    lhsT_scale=d_plane[:, t * P : (t + 1) * P],
+                    rhs=x_codes[u][:].bitcast(FP8X4),
+                    rhs_scale=x_plane[:, u * HALF : (u + 1) * HALF],
+                    start=True,
+                    stop=True,
+                )
+
+        h = [keep.tile([P, S], F32, name=f"h{t}") for t in range(PACK)]
+        sig = [keep.tile([P, W], F32, name=f"sig{t}") for t in range(PACK)]
+        ra = [keep.tile([P, W], F32, name=f"ra{t}", tag=f"ra{t}", align_bytes=64) for t in range(PACK)]
+        z_pairs = keep.tile([P, 2, S, 2], BF16, name="z_pairs", align_bytes=64)
+
+        def fetch_h(t):
+            for u in range(2):
+                nc.vector.tensor_copy(h[t][:, u * HALF : (u + 1) * HALF], h_acc[t, u][:])
+            nc.scalar.activation(sig[t][:], h[t][:].indirect(n2_t[:]), ACT.Sigmoid, scale=H_SCALE)
+
+        def gate_then_scalar_scatter(t):
+            nc.vector.tensor_tensor(ra[t][:], h[t][:].indirect(n1_t[:]), sig[t][:], ALU.mult)
+            nc.scalar.activation(h[t][:].indirect(n2_t[:]), ra[t][:], ACT.Copy)
+
+        def make_z(t):
+            nc.vector.tensor_scalar(z_pairs[:, t // 2, :, t % 2], h[t][:], gain[:, t : t + 1], H_SCALE, ALU.mult, ALU.mult)
+
+        fetch_h(0)
+        fetch_h(1)
+        gate_then_scalar_scatter(0)
+        fetch_h(2)
+        fetch_h(3)
+        gate_then_scalar_scatter(1)
+        nc.vector.tensor_copy(ra[3][:], h[3][:].indirect(n1_t[:]))
+        gate_then_scalar_scatter(2)
+        make_z(0)
+        nc.vector.tensor_tensor(h[3][:].indirect(n2_t[:]), ra[3][:], sig[3][:], ALU.mult)
+        make_z(1)
+        make_z(3)
+        make_z(2)
+
+        w_grouped = keep.tile([P, N, PACK], BF16, name="w_grouped", tag="ra2", align_bytes=64)
+        w_codes = keep.tile([P, N], U32, name="w_codes", align_bytes=64)
+        w_plane = keep.tile([P, N], U8, name="w_plane", align_bytes=64)
+
+        def round_w(m):
+            cols = slice(m * P, (m + 1) * P)
+            nc.scalar.copy(
+                w_grouped[:, cols, :].rearrange("p (c i) j -> p c j i", i=4),
+                w_raw[:, :, cols].rearrange("p j (c i) -> p c j i", i=4),
+            )
+
+        def quantise_w(m):
+            cols = slice(m * P, (m + 1) * P)
+            nc.vector.quantize_mx(
+                out=w_codes[:, cols].bitcast(FP8X4),
+                scales=w_plane[:, cols],
+                in_=w_grouped[:, cols, :].rearrange("p n j -> p (n j)"),
+            )
+
+        z_grouped = [keep.tile([P, HALF, PACK], BF16, name=f"z_grouped{u}", align_bytes=64) for u in range(2)]
+        z_codes = keep.tile([P, S], U32, name="z_codes", align_bytes=64)
+        z_plane = keep.tile([P, S], U8, name="z_plane", align_bytes=64)
+        z_words = z_pairs[:].rearrange("p v c e -> p v (c e)").bitcast(F32)
+        round_w(0)
+        for u in range(2):
+            nc.vector.tensor_copy(
+                z_grouped[u][:].rearrange("p c j -> p (c j)").bitcast(F32).rearrange("p (c v) -> p c v", v=2),
+                z_words[:, :, u * HALF : (u + 1) * HALF].rearrange("p v c -> p c v"),
+            )
+        quantise_w(0)
+        for u in range(2):
+            cols = slice(u * HALF, (u + 1) * HALF)
+            nc.vector.quantize_mx(
+                out=z_codes[:, cols].bitcast(FP8X4),
+                scales=z_plane[:, cols],
+                in_=z_grouped[u][:].rearrange("p c j -> p (c j)"),
+            )
+
+        def second_product(m, cols, bank):
+            acc = psum.tile([P, cols.stop - cols.start], F32, name=f"h2_acc{bank}", tag=f"bank{bank}")
+            nc.tensor.matmul_mx(
+                out=acc[:],
+                lhsT=w_codes[:, m * P : (m + 1) * P].bitcast(FP8X4),
+                lhsT_scale=w_plane[:, m * P : (m + 1) * P],
+                rhs=z_codes[:, cols].bitcast(FP8X4),
+                rhs_scale=z_plane[:, cols],
+                start=True,
+                stop=True,
+            )
+            return acc
+
+        first = [second_product(0, slice(u * HALF, (u + 1) * HALF), u) for u in range(2)]
+        nc.scalar.copy(h2[0][:, :HALF], first[0][:])
+        nc.vector.tensor_copy(h2[0][:, HALF:S], first[1][:])
+        h2_acc = {}
+        for m in range(1, N // P):
+            round_w(m)
+            quantise_w(m)
+            h2_acc[m] = second_product(m, slice(0, S), m + 1)
+
+        units = [(m, c, HALF) for m in range(N // P) for c in (0, HALF)]
+        units = units[:-1] + [(N // P - 1, HALF, P), (N // P - 1, HALF + P, P)]
+        on_vector = {(0, 0), (0, HALF)}
+
+        def gather(m, c, width):
+            mb = ring.tile([P, PACK * width], F32, name="mb", tag="mb")
+            for e in range(0, PACK * width, PIECE):
+                col = (PACK * c + e) // 16
+                window = h2[m][:].indirect(n3_t[:, col : col + PIECE // 16])
+                if e == 0 and (m, c) in on_vector:
+                    nc.vector.tensor_copy(mb[:, e : e + PIECE], window)
+                else:
+                    nc.scalar.activation(mb[:, e : e + PIECE], window, ACT.Copy)
+            return mb
+
+        def finish(m, c, width, mx, th, res):
+            nc.vector.tensor_tensor(res, mx[:], th[:], ALU.mult)
+            nc.sync.dma_start(out[m * P : (m + 1) * P, c : c + width], res)
+
+        waiting = []
+        for m, c, width in units:
+            if c == HALF and m + 1 < N // P:
+                nc.scalar.copy(h2[m + 1][:, :S], h2_acc[m + 1][:])
+            mb = gather(m, c, width)
+            four = mb[:].rearrange("p (j t) -> p j t", t=PACK)
+            hi = ring.tile([P, width, 2], F32, name="hi", tag="hi")
+            lo = ring.tile([P, width, 2], F32, name="lo", tag="lo")
+            mx = ring.tile([P, width], F32, name="mx", tag="mx", bufs=4)
+            mn = ring.tile([P, width], F32, name="mn", tag="mn")
+            gap = ring.tile([P, width], F32, name="gap", tag="gap")
+            th = ring.tile([P, width], F32, name="th", tag="th", bufs=4)
+            nc.vector.tensor_tensor(lo[:], four[:, :, 0:2], four[:, :, 2:4], ALU.min)
+            nc.vector.tensor_tensor(hi[:], four[:, :, 0:2], four[:, :, 2:4], ALU.max)
+            nc.vector.tensor_tensor(mn[:], lo[:, :, 0], lo[:, :, 1], ALU.min)
+            nc.vector.tensor_tensor(mx[:], hi[:, :, 0], hi[:, :, 1], ALU.max)
+            nc.vector.tensor_tensor(gap[:], h2[m][:, c : c + width], mn[:], ALU.subtract)
+            nc.scalar.activation(th[:], gap[:], ACT.Tanh)
+            waiting.append((m, c, width, mx, th))
+            if len(waiting) > 2:
+                finish(*waiting[-3], hi[:].rearrange("p j e -> p (j e)")[:, : waiting[-3][2]])
+        for i, unit in enumerate(waiting[-2:]):
+            last = keep.tile([P, P], F32, name=f"last{i}")
+            finish(*unit, last[:])

@@ -20,6 +20,7 @@ PACK = 4
 HALF = S // 2
 PIECE = 512
 SPARE = 16
+LAG = 2
 H_SCALE = 0.0625
 
 
@@ -43,17 +44,16 @@ def tile_picked_pqlayfoldgtan_none_p_kernel(
             nc.sync.dma_start(tile[:].bitcast(I32), src[0].rearrange("p n t -> p (n t)").bitcast(I32))
             return tile
 
-        k1_t = load_list(k1, "k1_t")
         d_rows = keep.tile([P, G], U8, name="d_rows", align_bytes=64)
-        nc.sync.dma_start(
-            d_rows[:].bitcast(I32), d_scales[0].bitcast(I32).unsqueeze(1).broadcast_to([16, 8, G // 4])
-        )
-        offs_t = load_list(offs, "offs_t")
-        d_table = load_words(d_words, "d_table")
+        nc.vector.memset(d_rows[:].bitcast(I32), 0)
         x_rows = keep.tile([P, T], U8, name="x_rows", align_bytes=64)
         nc.vector.memset(x_rows[:].bitcast(I32), 0)
+        k1_t = load_list(k1, "k1_t")
+        offs_t = load_list(offs, "offs_t")
+        nc.sync.dma_start(d_rows[0:P:8, :].bitcast(I32), d_scales[0].bitcast(I32))
         for q in range(4):
-            nc.scalar.dma_start(x_rows[32 * q : 32 * q + 4, :].bitcast(I32), x_scales[0, 4 * q : 4 * (q + 1), :].bitcast(I32))
+            nc.sync.dma_start(x_rows[32 * q : 32 * q + 4, :].bitcast(I32), x_scales[0, 4 * q : 4 * (q + 1), :].bitcast(I32))
+        d_table = load_words(d_words, "d_table")
         x_table = load_words(x_words, "x_table")
         n2_t = load_list(n2, "n2_t")
         n1_t = load_list(n1, "n1_t")
@@ -69,15 +69,18 @@ def tile_picked_pqlayfoldgtan_none_p_kernel(
         nc.vector.tensor_copy(d_bytes[:], d_rows[:].indirect(k1_t[:]))
         d_dealt = keep.tile([P, H], U8, name="d_dealt", tag="w_raw", align_bytes=64)
         nc.vector.tensor_copy(
-            d_dealt[:].rearrange("p (t m) -> p m t", t=PACK), d_bytes[:].rearrange("p (m t) -> p m t", t=PACK)
+            d_dealt[:].rearrange("p (t m) -> p t m", t=PACK), d_bytes[:].rearrange("p (m t) -> p t m", t=PACK)
         )
         for q in range(4):
             nc.scalar.dma_start(
                 d_plane[32 * q : 32 * q + 4, :].bitcast(I32), d_dealt[32 * q : 32 * (q + 1) : 8, :].bitcast(I32)
             )
 
+        x_plane = keep.tile([P, S], U8, name="x_plane", align_bytes=64)
+        nc.vector.tensor_copy(x_plane[:], x_rows[:].indirect(offs_t[:]))
+
         w_raw = keep.tile([P, PACK, N], F32, name="w_raw", tag="w_raw", align_bytes=64)
-        nc.sync.dma_start(w_raw[:], w1.rearrange("(p j) n -> p j n", j=PACK))
+        nc.scalar.dma_start(w_raw[:], w1.rearrange("(p j) n -> p j n", j=PACK))
 
         d_picked = keep.tile([P, H], U32, name="d_picked", tag="gain", align_bytes=64)
         nc.vector.tensor_copy(d_picked[:], d_table[:].indirect(k1_t[:]))
@@ -86,8 +89,6 @@ def tile_picked_pqlayfoldgtan_none_p_kernel(
             d_codes[:].bitcast(I32).rearrange("p (t m) -> p m t", t=PACK),
             d_picked[:].bitcast(I32).rearrange("p (m t) -> p m t", t=PACK),
         )
-        x_plane = keep.tile([P, S], U8, name="x_plane", align_bytes=64)
-        nc.vector.tensor_copy(x_plane[:], x_rows[:].indirect(offs_t[:]))
         gain = keep.tile([P, PACK], F32, name="gain", tag="gain", align_bytes=64)
         nc.sync.dma_start(gain[:], gn.rearrange("(p t) o -> p (t o)", t=PACK))
         x_codes = [keep.tile([P, HALF], U32, name=f"x_codes{u}", align_bytes=64) for u in range(2)]
@@ -110,7 +111,7 @@ def tile_picked_pqlayfoldgtan_none_p_kernel(
         h = [keep.tile([P, S], F32, name=f"h{t}") for t in range(PACK)]
         sig = [keep.tile([P, W], F32, name=f"sig{t}") for t in range(PACK)]
         ra = [keep.tile([P, W], F32, name=f"ra{t}", tag=f"ra{t}", align_bytes=64) for t in range(PACK)]
-        z_pairs = keep.tile([P, 2, S, 2], BF16, name="z_pairs", align_bytes=64)
+        z_pairs = [keep.tile([P, 2, HALF, 2], BF16, name=f"z_pairs{u}", align_bytes=64) for u in range(2)]
 
         def fetch_h(t):
             for u in range(2):
@@ -122,7 +123,30 @@ def tile_picked_pqlayfoldgtan_none_p_kernel(
             nc.scalar.activation(h[t][:].indirect(n2_t[:]), ra[t][:], ACT.Copy)
 
         def make_z(t):
-            nc.vector.tensor_scalar(z_pairs[:, t // 2, :, t % 2], h[t][:], gain[:, t : t + 1], H_SCALE, ALU.mult, ALU.mult)
+            for u in range(2):
+                nc.vector.tensor_scalar(
+                    z_pairs[u][:, t // 2, :, t % 2],
+                    h[t][:, u * HALF : (u + 1) * HALF],
+                    gain[:, t : t + 1],
+                    H_SCALE,
+                    ALU.mult,
+                    ALU.mult,
+                )
+
+        w_codes = keep.tile([P, N], U32, name="w_codes", align_bytes=64)
+        w_plane = keep.tile([P, N], U8, name="w_plane", align_bytes=64)
+
+        def round_w(copy, grouped, m):
+            copy(
+                grouped.rearrange("p (c i) j -> p c j i", i=4),
+                w_raw[:, :, m * P : (m + 1) * P].rearrange("p j (c i) -> p c j i", i=4),
+            )
+
+        def quantise_w(grouped, m):
+            cols = slice(m * P, (m + 1) * P)
+            nc.vector.quantize_mx(
+                out=w_codes[:, cols].bitcast(FP8X4), scales=w_plane[:, cols], in_=grouped.rearrange("p n j -> p (n j)")
+            )
 
         fetch_h(0)
         fetch_h(1)
@@ -135,39 +159,21 @@ def tile_picked_pqlayfoldgtan_none_p_kernel(
         make_z(0)
         nc.vector.tensor_tensor(h[3][:].indirect(n2_t[:]), ra[3][:], sig[3][:], ALU.mult)
         make_z(1)
+        w_first = keep.tile([P, P, PACK], BF16, name="w_first", tag="ra3", align_bytes=64)
+        round_w(nc.vector.tensor_copy, w_first[:], 0)
         make_z(3)
+        quantise_w(w_first[:], 0)
         make_z(2)
-
-        w_grouped = keep.tile([P, N, PACK], BF16, name="w_grouped", tag="ra2", align_bytes=64)
-        w_codes = keep.tile([P, N], U32, name="w_codes", align_bytes=64)
-        w_plane = keep.tile([P, N], U8, name="w_plane", align_bytes=64)
-
-        def round_w(m):
-            cols = slice(m * P, (m + 1) * P)
-            nc.scalar.copy(
-                w_grouped[:, cols, :].rearrange("p (c i) j -> p c j i", i=4),
-                w_raw[:, :, cols].rearrange("p j (c i) -> p c j i", i=4),
-            )
-
-        def quantise_w(m):
-            cols = slice(m * P, (m + 1) * P)
-            nc.vector.quantize_mx(
-                out=w_codes[:, cols].bitcast(FP8X4),
-                scales=w_plane[:, cols],
-                in_=w_grouped[:, cols, :].rearrange("p n j -> p (n j)"),
-            )
+        w_rest = keep.tile([P, N - P, PACK], BF16, name="w_rest", tag="ra2", align_bytes=64)
 
         z_grouped = [keep.tile([P, HALF, PACK], BF16, name=f"z_grouped{u}", align_bytes=64) for u in range(2)]
         z_codes = keep.tile([P, S], U32, name="z_codes", align_bytes=64)
         z_plane = keep.tile([P, S], U8, name="z_plane", align_bytes=64)
-        z_words = z_pairs[:].rearrange("p v c e -> p v (c e)").bitcast(F32)
-        round_w(0)
         for u in range(2):
             nc.vector.tensor_copy(
                 z_grouped[u][:].rearrange("p c j -> p (c j)").bitcast(F32).rearrange("p (c v) -> p c v", v=2),
-                z_words[:, :, u * HALF : (u + 1) * HALF].rearrange("p v c -> p c v"),
+                z_pairs[u][:].rearrange("p v c e -> p v (c e)").bitcast(F32).rearrange("p v c -> p c v"),
             )
-        quantise_w(0)
         for u in range(2):
             cols = slice(u * HALF, (u + 1) * HALF)
             nc.vector.quantize_mx(
@@ -194,50 +200,50 @@ def tile_picked_pqlayfoldgtan_none_p_kernel(
         nc.vector.tensor_copy(h2[0][:, HALF:S], first[1][:])
         h2_acc = {}
         for m in range(1, N // P):
-            round_w(m)
-            quantise_w(m)
-            h2_acc[m] = second_product(m, slice(0, S), m + 1)
+            round_w(nc.scalar.copy, w_rest[:, (m - 1) * P : m * P, :], m)
+            quantise_w(w_rest[:, (m - 1) * P : m * P, :], m)
+            h2_acc[m] = second_product(m, slice(0, S), m)
 
-        units = [(m, c, HALF) for m in range(N // P) for c in (0, HALF)]
-        units = units[:-1] + [(N // P - 1, HALF, P), (N // P - 1, HALF + P, P)]
-        on_vector = {(0, 0), (0, HALF)}
+        units = [(m, c) for m in range(N // P) for c in (0, HALF)]
+        vector_share = [PIECE, PIECE, PIECE // 2]
 
-        def gather(m, c, width):
-            mb = ring.tile([P, PACK * width], F32, name="mb", tag="mb")
-            for e in range(0, PACK * width, PIECE):
-                col = (PACK * c + e) // 16
-                window = h2[m][:].indirect(n3_t[:, col : col + PIECE // 16])
-                if e == 0 and (m, c) in on_vector:
-                    nc.vector.tensor_copy(mb[:, e : e + PIECE], window)
+        def gather(k, m, c):
+            mb = ring.tile([P, PACK * HALF], F32, name="mb", tag="mb")
+            share = vector_share[k] if k < len(vector_share) else 0
+            cuts = sorted({0, share, PIECE, PACK * HALF})
+            for lo_e, hi_e in zip(cuts, cuts[1:]):
+                window = h2[m][:].indirect(n3_t[:, (PACK * c + lo_e) // 16 : (PACK * c + hi_e) // 16])
+                if hi_e <= share:
+                    nc.vector.tensor_copy(mb[:, lo_e:hi_e], window)
                 else:
-                    nc.scalar.activation(mb[:, e : e + PIECE], window, ACT.Copy)
+                    nc.scalar.activation(mb[:, lo_e:hi_e], window, ACT.Copy)
             return mb
 
-        def finish(m, c, width, mx, th, res):
+        def finish(m, c, mx, th, res):
             nc.vector.tensor_tensor(res, mx[:], th[:], ALU.mult)
-            nc.sync.dma_start(out[m * P : (m + 1) * P, c : c + width], res)
+            nc.sync.dma_start(out[m * P : (m + 1) * P, c : c + HALF], res)
 
         waiting = []
-        for m, c, width in units:
+        for k, (m, c) in enumerate(units):
             if c == HALF and m + 1 < N // P:
                 nc.scalar.copy(h2[m + 1][:, :S], h2_acc[m + 1][:])
-            mb = gather(m, c, width)
+            mb = gather(k, m, c)
             four = mb[:].rearrange("p (j t) -> p j t", t=PACK)
-            hi = ring.tile([P, width, 2], F32, name="hi", tag="hi")
-            lo = ring.tile([P, width, 2], F32, name="lo", tag="lo")
-            mx = ring.tile([P, width], F32, name="mx", tag="mx", bufs=4)
-            mn = ring.tile([P, width], F32, name="mn", tag="mn")
-            gap = ring.tile([P, width], F32, name="gap", tag="gap")
-            th = ring.tile([P, width], F32, name="th", tag="th", bufs=4)
+            hi = ring.tile([P, HALF, 2], F32, name="hi", tag="hi")
+            lo = ring.tile([P, HALF, 2], F32, name="lo", tag="lo")
+            mx = ring.tile([P, HALF], F32, name="mx", tag="mx", bufs=LAG + 2)
+            mn = ring.tile([P, HALF], F32, name="mn", tag="mn")
+            gap = ring.tile([P, HALF], F32, name="gap", tag="gap", bufs=LAG + 2)
+            th = ring.tile([P, HALF], F32, name="th", tag="th", bufs=LAG + 2)
             nc.vector.tensor_tensor(lo[:], four[:, :, 0:2], four[:, :, 2:4], ALU.min)
             nc.vector.tensor_tensor(hi[:], four[:, :, 0:2], four[:, :, 2:4], ALU.max)
             nc.vector.tensor_tensor(mn[:], lo[:, :, 0], lo[:, :, 1], ALU.min)
             nc.vector.tensor_tensor(mx[:], hi[:, :, 0], hi[:, :, 1], ALU.max)
-            nc.vector.tensor_tensor(gap[:], h2[m][:, c : c + width], mn[:], ALU.subtract)
+            nc.vector.tensor_tensor(gap[:], h2[m][:, c : c + HALF], mn[:], ALU.subtract)
             nc.scalar.activation(th[:], gap[:], ACT.Tanh)
-            waiting.append((m, c, width, mx, th))
-            if len(waiting) > 2:
-                finish(*waiting[-3], hi[:].rearrange("p j e -> p (j e)")[:, : waiting[-3][2]])
-        for i, unit in enumerate(waiting[-2:]):
-            last = keep.tile([P, P], F32, name=f"last{i}")
+            waiting.append((m, c, mx, th))
+            if k >= LAG:
+                finish(*waiting[k - LAG], hi[:].rearrange("p j e -> p (j e)")[:, :HALF])
+        for i, unit in enumerate(waiting[-LAG:]):
+            last = keep.tile([P, HALF], F32, name=f"last{i}")
             finish(*unit, last[:])

@@ -20,7 +20,7 @@ PACK = 4
 HALF = S // 2
 PIECE = 512
 SPARE = 16
-LAG = 2
+LAG = 3
 H_SCALE = 0.0625
 
 
@@ -91,31 +91,36 @@ def tile_picked_pqlayfoldgtan_none_p_kernel(
         )
         gain = keep.tile([P, PACK], F32, name="gain", tag="gain", align_bytes=64)
         nc.sync.dma_start(gain[:], gn.rearrange("(p t) o -> p (t o)", t=PACK))
-        x_codes = [keep.tile([P, HALF], U32, name=f"x_codes{u}", align_bytes=64) for u in range(2)]
-        for u in range(2):
-            nc.vector.tensor_copy(x_codes[u][:], x_table[:].indirect(offs_t[:, u * HALF // 16 : (u + 1) * HALF // 16]))
+        x_codes = keep.tile([P, S], U32, name="x_codes", align_bytes=64)
+        x_cuts = [slice(0, HALF), slice(HALF, HALF + P), slice(HALF + P, S)]
+        for cols in x_cuts:
+            nc.vector.tensor_copy(x_codes[:, cols], x_table[:].indirect(offs_t[:, cols.start // 16 : cols.stop // 16]))
         h_acc = {}
+        banks = list(range(8))
         for t in range(PACK):
-            for u in range(2):
-                h_acc[t, u] = psum.tile([P, HALF], F32, name=f"h_acc{t}{u}", tag=f"bank{2 * t + u}")
+            h_acc[t] = []
+            for cols in x_cuts if t == 0 else [slice(0, S)]:
+                bank = banks.pop(0)
+                acc = psum.tile([P, cols.stop - cols.start], F32, name=f"h_acc{bank}", tag=f"bank{bank}")
                 nc.tensor.matmul_mx(
-                    out=h_acc[t, u][:],
+                    out=acc[:],
                     lhsT=d_codes[:, t * P : (t + 1) * P].bitcast(FP8X4),
                     lhsT_scale=d_plane[:, t * P : (t + 1) * P],
-                    rhs=x_codes[u][:].bitcast(FP8X4),
-                    rhs_scale=x_plane[:, u * HALF : (u + 1) * HALF],
+                    rhs=x_codes[:, cols].bitcast(FP8X4),
+                    rhs_scale=x_plane[:, cols],
                     start=True,
                     stop=True,
                 )
+                h_acc[t].append((cols, acc))
 
         h = [keep.tile([P, S], F32, name=f"h{t}") for t in range(PACK)]
         sig = [keep.tile([P, W], F32, name=f"sig{t}") for t in range(PACK)]
         ra = [keep.tile([P, W], F32, name=f"ra{t}", tag=f"ra{t}", align_bytes=64) for t in range(PACK)]
-        z_pairs = [keep.tile([P, 2, HALF, 2], BF16, name=f"z_pairs{u}", align_bytes=64) for u in range(2)]
+        z_pairs = [keep.tile([P, 2, HALF, 2], BF16, name=f"z_pairs{u}", tag=f"z_pairs{u}", align_bytes=64) for u in range(2)]
 
         def fetch_h(t):
-            for u in range(2):
-                nc.vector.tensor_copy(h[t][:, u * HALF : (u + 1) * HALF], h_acc[t, u][:])
+            for cols, acc in h_acc[t]:
+                nc.vector.tensor_copy(h[t][:, cols], acc[:])
             nc.scalar.activation(sig[t][:], h[t][:].indirect(n2_t[:]), ACT.Sigmoid, scale=H_SCALE)
 
         def gate_then_scalar_scatter(t):
@@ -133,19 +138,20 @@ def tile_picked_pqlayfoldgtan_none_p_kernel(
                     ALU.mult,
                 )
 
-        w_codes = keep.tile([P, N], U32, name="w_codes", align_bytes=64)
         w_plane = keep.tile([P, N], U8, name="w_plane", align_bytes=64)
 
-        def round_w(copy, grouped, m):
-            copy(
-                grouped.rearrange("p (c i) j -> p c j i", i=4),
+        def round_w(m):
+            nc.scalar.copy(
+                w_grouped[:, m * P : (m + 1) * P, :].rearrange("p (c i) j -> p c j i", i=4),
                 w_raw[:, :, m * P : (m + 1) * P].rearrange("p j (c i) -> p c j i", i=4),
             )
 
-        def quantise_w(grouped, m):
+        def quantise_w(m):
             cols = slice(m * P, (m + 1) * P)
             nc.vector.quantize_mx(
-                out=w_codes[:, cols].bitcast(FP8X4), scales=w_plane[:, cols], in_=grouped.rearrange("p n j -> p (n j)")
+                out=w_codes[:, cols].bitcast(FP8X4),
+                scales=w_plane[:, cols],
+                in_=w_grouped[:, cols, :].rearrange("p n j -> p (n j)"),
             )
 
         fetch_h(0)
@@ -159,12 +165,10 @@ def tile_picked_pqlayfoldgtan_none_p_kernel(
         make_z(0)
         nc.vector.tensor_tensor(h[3][:].indirect(n2_t[:]), ra[3][:], sig[3][:], ALU.mult)
         make_z(1)
-        w_first = keep.tile([P, P, PACK], BF16, name="w_first", tag="ra3", align_bytes=64)
-        round_w(nc.vector.tensor_copy, w_first[:], 0)
         make_z(3)
-        quantise_w(w_first[:], 0)
         make_z(2)
-        w_rest = keep.tile([P, N - P, PACK], BF16, name="w_rest", tag="ra2", align_bytes=64)
+        w_grouped = keep.tile([P, N, PACK], BF16, name="w_grouped", tag="ra2", align_bytes=64)
+        round_w(0)
 
         z_grouped = [keep.tile([P, HALF, PACK], BF16, name=f"z_grouped{u}", align_bytes=64) for u in range(2)]
         z_codes = keep.tile([P, S], U32, name="z_codes", align_bytes=64)
@@ -174,6 +178,8 @@ def tile_picked_pqlayfoldgtan_none_p_kernel(
                 z_grouped[u][:].rearrange("p c j -> p (c j)").bitcast(F32).rearrange("p (c v) -> p c v", v=2),
                 z_pairs[u][:].rearrange("p v c e -> p v (c e)").bitcast(F32).rearrange("p v c -> p c v"),
             )
+        w_codes = keep.tile([P, N], U32, name="w_codes", tag="z_pairs1", align_bytes=64)
+        quantise_w(0)
         for u in range(2):
             cols = slice(u * HALF, (u + 1) * HALF)
             nc.vector.quantize_mx(
@@ -200,12 +206,12 @@ def tile_picked_pqlayfoldgtan_none_p_kernel(
         nc.vector.tensor_copy(h2[0][:, HALF:S], first[1][:])
         h2_acc = {}
         for m in range(1, N // P):
-            round_w(nc.scalar.copy, w_rest[:, (m - 1) * P : m * P, :], m)
-            quantise_w(w_rest[:, (m - 1) * P : m * P, :], m)
+            round_w(m)
+            quantise_w(m)
             h2_acc[m] = second_product(m, slice(0, S), m)
 
         units = [(m, c) for m in range(N // P) for c in (0, HALF)]
-        vector_share = [PIECE, PIECE, PIECE // 2]
+        vector_share = [PIECE, PIECE, PIECE]
 
         def gather(k, m, c):
             mb = ring.tile([P, PACK * HALF], F32, name="mb", tag="mb")

@@ -211,7 +211,7 @@ def tile_picked_pqlayfoldgtan_none_p_kernel(
             h2_acc[m] = second_product(m, slice(0, S), m)
 
         units = [(m, c) for m in range(N // P) for c in (0, HALF)]
-        vector_share = [PIECE, PIECE, PIECE]
+        vector_share = [PIECE, PIECE, PIECE // 2]
 
         def gather(k, m, c):
             mb = ring.tile([P, PACK * HALF], F32, name="mb", tag="mb")
@@ -235,21 +235,21 @@ def tile_picked_pqlayfoldgtan_none_p_kernel(
                 nc.scalar.copy(h2[m + 1][:, :S], h2_acc[m + 1][:])
             mb = gather(k, m, c)
             four = mb[:].rearrange("p (j t) -> p j t", t=PACK)
-            hi = ring.tile([P, HALF, 2], F32, name="hi", tag="hi")
-            lo = ring.tile([P, HALF, 2], F32, name="lo", tag="lo")
+            hi = ring.tile([P, 2, HALF], F32, name="hi", tag="hi")
+            lo = ring.tile([P, 2, HALF], F32, name="lo", tag="lo")
             mx = ring.tile([P, HALF], F32, name="mx", tag="mx", bufs=LAG + 2)
             mn = ring.tile([P, HALF], F32, name="mn", tag="mn")
             gap = ring.tile([P, HALF], F32, name="gap", tag="gap", bufs=LAG + 2)
             th = ring.tile([P, HALF], F32, name="th", tag="th", bufs=LAG + 2)
-            nc.vector.tensor_tensor(lo[:], four[:, :, 0:2], four[:, :, 2:4], ALU.min)
-            nc.vector.tensor_tensor(hi[:], four[:, :, 0:2], four[:, :, 2:4], ALU.max)
-            nc.vector.tensor_tensor(mn[:], lo[:, :, 0], lo[:, :, 1], ALU.min)
-            nc.vector.tensor_tensor(mx[:], hi[:, :, 0], hi[:, :, 1], ALU.max)
+            nc.vector.tensor_tensor(lo[:].rearrange("p e j -> p j e"), four[:, :, 0:2], four[:, :, 2:4], ALU.min)
+            nc.vector.tensor_tensor(hi[:].rearrange("p e j -> p j e"), four[:, :, 0:2], four[:, :, 2:4], ALU.max)
+            nc.vector.tensor_tensor(mn[:], lo[:, 0, :], lo[:, 1, :], ALU.min)
+            nc.vector.tensor_tensor(mx[:], hi[:, 0, :], hi[:, 1, :], ALU.max)
             nc.vector.tensor_tensor(gap[:], h2[m][:, c : c + HALF], mn[:], ALU.subtract)
             nc.scalar.activation(th[:], gap[:], ACT.Tanh)
             waiting.append((m, c, mx, th))
             if k >= LAG:
-                finish(*waiting[k - LAG], hi[:].rearrange("p j e -> p (j e)")[:, :HALF])
+                finish(*waiting[k - LAG], hi[:, 0, :])
         for i, unit in enumerate(waiting[-LAG:]):
             last = keep.tile([P, HALF], F32, name=f"last{i}")
             finish(*unit, last[:])

from contextlib import ExitStack

import concourse.mybir as mybir

K, T, S, N, G, H, W = 512, 2048, 512, 512, 2048, 512, 256
FLOPS = 2 * K * H * S + 2 * H * N * S

F32 = mybir.dt.float32
BF16 = mybir.dt.bfloat16
I32 = mybir.dt.int32
U32 = mybir.dt.uint32
U16 = mybir.dt.uint16
U8 = mybir.dt.uint8
FP8X4 = mybir.dt.float8_e4m3fn_x4
ALU = mybir.AluOpType
ACT = mybir.ActivationFunctionType

P = 128
PACK = 4
HALF = S // 2
PIECE = 512
SPARE = 16
LAG = 3
H_SCALE = 0.0625


def tile_picked_pqlayfoldgtan_none_p_kernel(
    tc, x_words, x_scales, d_words, d_scales, gn, w1, offs, k1, n1, n2, n3, out
):
    nc = tc.nc
    with ExitStack() as ctx:
        lists = ctx.enter_context(tc.tile_pool(name="lists", bufs=1))
        keep = ctx.enter_context(tc.tile_pool(name="keep", bufs=1))
        ring = ctx.enter_context(tc.tile_pool(name="ring", bufs=3))
        psum = ctx.enter_context(tc.psum_pool(name="psum", bufs=1))

        def load_list(src, name):
            tile = lists.tile([P, src.shape[1]], U16, name=name)
            nc.sync.dma_start(tile[:], src)
            return tile

        def load_words(src, name):
            tile = keep.tile([P, src.shape[2]], U32, name=name, align_bytes=64)
            nc.sync.dma_start(tile[:].bitcast(I32), src[0].rearrange("p n t -> p (n t)").bitcast(I32))
            return tile

        d_rows = keep.tile([P, G], U8, name="d_rows", align_bytes=64)
        nc.vector.memset(d_rows[:].bitcast(I32), 0)
        x_rows = keep.tile([P, T], U8, name="x_rows", align_bytes=64)
        nc.vector.memset(x_rows[:].bitcast(I32), 0)
        k1_t = load_list(k1, "k1_t")
        offs_t = load_list(offs, "offs_t")
        nc.sync.dma_start(d_rows[0:P:8, :].bitcast(I32), d_scales[0].bitcast(I32))
        for q in range(4):
            nc.sync.dma_start(x_rows[32 * q : 32 * q + 4, :].bitcast(I32), x_scales[0, 4 * q : 4 * (q + 1), :].bitcast(I32))
        d_table = load_words(d_words, "d_table")
        x_table = load_words(x_words, "x_table")
        n2_t = load_list(n2, "n2_t")
        n1_t = load_list(n1, "n1_t")
        n3_t = load_list(n3, "n3_t")

        d_plane = keep.tile([P, H], U8, name="d_plane", align_bytes=64)
        nc.vector.memset(d_plane[:].bitcast(I32), 0)
        h2 = [keep.tile([P, S + SPARE], F32, name=f"h2_{m}") for m in range(N // P)]
        for m in range(N // P):
            nc.vector.memset(h2[m][:, S:], 0.0)

        d_bytes = keep.tile([P, H], U8, name="d_bytes", align_bytes=64)
        nc.vector.tensor_copy(d_bytes[:], d_rows[:].indirect(k1_t[:]))
        d_dealt = keep.tile([P, H], U8, name="d_dealt", tag="w_raw", align_bytes=64)
        nc.vector.tensor_copy(
            d_dealt[:].rearrange("p (t m) -> p t m", t=PACK), d_bytes[:].rearrange("p (m t) -> p t m", t=PACK)
        )
        for q in range(4):
            nc.scalar.dma_start(
                d_plane[32 * q : 32 * q + 4, :].bitcast(I32), d_dealt[32 * q : 32 * (q + 1) : 8, :].bitcast(I32)
            )

        x_plane = keep.tile([P, S], U8, name="x_plane", align_bytes=64)
        nc.vector.tensor_copy(x_plane[:], x_rows[:].indirect(offs_t[:]))

        w_raw = keep.tile([P, PACK, N], F32, name="w_raw", tag="w_raw", align_bytes=64)
        nc.scalar.dma_start(w_raw[:], w1.rearrange("(p j) n -> p j n", j=PACK))

        d_picked = keep.tile([P, H], U32, name="d_picked", tag="gain", align_bytes=64)
        nc.vector.tensor_copy(d_picked[:], d_table[:].indirect(k1_t[:]))
        d_codes = keep.tile([P, H], U32, name="d_codes", align_bytes=64)
        nc.vector.tensor_copy(
            d_codes[:].bitcast(I32).rearrange("p (t m) -> p m t", t=PACK),
            d_picked[:].bitcast(I32).rearrange("p (m t) -> p m t", t=PACK),
        )
        gain = keep.tile([P, PACK], F32, name="gain", tag="gain", align_bytes=64)
        nc.sync.dma_start(gain[:], gn.rearrange("(p t) o -> p (t o)", t=PACK))
        x_codes = keep.tile([P, S], U32, name="x_codes", align_bytes=64)
        x_cuts = [slice(0, HALF), slice(HALF, HALF + P), slice(HALF + P, S)]
        for cols in x_cuts:
            nc.vector.tensor_copy(x_codes[:, cols], x_table[:].indirect(offs_t[:, cols.start // 16 : cols.stop // 16]))
        h_acc = {}
        banks = list(range(8))
        for t in range(PACK):
            h_acc[t] = []
            for cols in x_cuts if t == 0 else [slice(0, S)]:
                bank = banks.pop(0)
                acc = psum.tile([P, cols.stop - cols.start], F32, name=f"h_acc{bank}", tag=f"bank{bank}")
                nc.tensor.matmul_mx(
                    out=acc[:],
                    lhsT=d_codes[:, t * P : (t + 1) * P].bitcast(FP8X4),
                    lhsT_scale=d_plane[:, t * P : (t + 1) * P],
                    rhs=x_codes[:, cols].bitcast(FP8X4),
                    rhs_scale=x_plane[:, cols],
                    start=True,
                    stop=True,
                )
                h_acc[t].append((cols, acc))

        h = [keep.tile([P, S], F32, name=f"h{t}") for t in range(PACK)]
        sig = [keep.tile([P, W], F32, name=f"sig{t}") for t in range(PACK)]
        ra = [keep.tile([P, W], F32, name=f"ra{t}", tag=f"ra{t}", align_bytes=64) for t in range(PACK)]
        z_pairs = [keep.tile([P, 2, HALF, 2], BF16, name=f"z_pairs{u}", tag=f"z_pairs{u}", align_bytes=64) for u in range(2)]

        def fetch_h(t):
            for cols, acc in h_acc[t]:
                nc.vector.tensor_copy(h[t][:, cols], acc[:])
            nc.scalar.activation(sig[t][:], h[t][:].indirect(n2_t[:]), ACT.Sigmoid, scale=H_SCALE)

        def gate_then_scalar_scatter(t):
            nc.vector.tensor_tensor(ra[t][:], h[t][:].indirect(n1_t[:]), sig[t][:], ALU.mult)
            nc.scalar.activation(h[t][:].indirect(n2_t[:]), ra[t][:], ACT.Copy)

        def make_z(t):
            for u in range(2):
                nc.vector.tensor_scalar(
                    z_pairs[u][:, t // 2, :, t % 2],
                    h[t][:, u * HALF : (u + 1) * HALF],
                    gain[:, t : t + 1],
                    H_SCALE,
                    ALU.mult,
                    ALU.mult,
                )

        w_plane = keep.tile([P, N], U8, name="w_plane", align_bytes=64)

        def round_w(m):
            nc.scalar.copy(
                w_grouped[:, m * P : (m + 1) * P, :].rearrange("p (c i) j -> p c j i", i=4),
                w_raw[:, :, m * P : (m + 1) * P].rearrange("p j (c i) -> p c j i", i=4),
            )

        def quantise_w(m):
            cols = slice(m * P, (m + 1) * P)
            nc.vector.quantize_mx(
                out=w_codes[:, cols].bitcast(FP8X4),
                scales=w_plane[:, cols],
                in_=w_grouped[:, cols, :].rearrange("p n j -> p (n j)"),
            )

        fetch_h(0)
        fetch_h(1)
        gate_then_scalar_scatter(0)
        fetch_h(2)
        fetch_h(3)
        gate_then_scalar_scatter(1)
        nc.vector.tensor_copy(ra[3][:], h[3][:].indirect(n1_t[:]))
        gate_then_scalar_scatter(2)
        make_z(0)
        nc.vector.tensor_tensor(h[3][:].indirect(n2_t[:]), ra[3][:], sig[3][:], ALU.mult)
        make_z(1)
        make_z(3)
        make_z(2)
        w_grouped = keep.tile([P, N, PACK], BF16, name="w_grouped", tag="ra2", align_bytes=64)
        round_w(0)

        z_grouped = [keep.tile([P, HALF, PACK], BF16, name=f"z_grouped{u}", align_bytes=64) for u in range(2)]
        z_codes = keep.tile([P, S], U32, name="z_codes", align_bytes=64)
        z_plane = keep.tile([P, S], U8, name="z_plane", align_bytes=64)
        for u in range(2):
            nc.vector.tensor_copy(
                z_grouped[u][:].rearrange("p c j -> p (c j)").bitcast(F32).rearrange("p (c v) -> p c v", v=2),
                z_pairs[u][:].rearrange("p v c e -> p v (c e)").bitcast(F32).rearrange("p v c -> p c v"),
            )
        w_codes = keep.tile([P, N], U32, name="w_codes", tag="z_pairs1", align_bytes=64)
        quantise_w(0)
        for u in range(2):
            cols = slice(u * HALF, (u + 1) * HALF)
            nc.vector.quantize_mx(
                out=z_codes[:, cols].bitcast(FP8X4),
                scales=z_plane[:, cols],
                in_=z_grouped[u][:].rearrange("p c j -> p (c j)"),
            )

        def second_product(m, cols, bank):
            acc = psum.tile([P, cols.stop - cols.start], F32, name=f"h2_acc{bank}", tag=f"bank{bank}")
            nc.tensor.matmul_mx(
                out=acc[:],
                lhsT=w_codes[:, m * P : (m + 1) * P].bitcast(FP8X4),
                lhsT_scale=w_plane[:, m * P : (m + 1) * P],
                rhs=z_codes[:, cols].bitcast(FP8X4),
                rhs_scale=z_plane[:, cols],
                start=True,
                stop=True,
            )
            return acc

        first = [second_product(0, slice(u * HALF, (u + 1) * HALF), u) for u in range(2)]
        nc.scalar.copy(h2[0][:, :HALF], first[0][:])
        nc.vector.tensor_copy(h2[0][:, HALF:S], first[1][:])
        h2_acc = {}
        for m in range(1, N // P):
            round_w(m)
            quantise_w(m)
            h2_acc[m] = second_product(m, slice(0, S), m)

        units = [(m, c) for m in range(N // P) for c in (0, HALF)]
        vector_share = [PIECE, PIECE, PIECE // 2]

        def gather(k, m, c):
            mb = ring.tile([P, PACK * HALF], F32, name="mb", tag="mb")
            share = vector_share[k] if k < len(vector_share) else 0
            cuts = sorted({0, share, PIECE, PACK * HALF})
            for lo_e, hi_e in zip(cuts, cuts[1:]):
                window = h2[m][:].indirect(n3_t[:, (PACK * c + lo_e) // 16 : (PACK * c + hi_e) // 16])
                if hi_e <= share:
                    nc.vector.tensor_copy(mb[:, lo_e:hi_e], window)
                else:
                    nc.scalar.activation(mb[:, lo_e:hi_e], window, ACT.Copy)
            return mb

        def finish(m, c, mx, th, res):
            nc.vector.tensor_tensor(res, mx[:], th[:], ALU.mult)
            nc.sync.dma_start(out[m * P : (m + 1) * P, c : c + HALF], res)

        waiting = []
        for k, (m, c) in enumerate(units):
            if c == HALF and m + 1 < N // P:
                nc.scalar.copy(h2[m + 1][:, :S], h2_acc[m + 1][:])
            mb = gather(k, m, c)
            four = mb[:].rearrange("p (j t) -> p j t", t=PACK)
            hi = ring.tile([P, 2, HALF], F32, name="hi", tag="hi")
            lo = ring.tile([P, 2, HALF], F32, name="lo", tag="lo")
            mx = ring.tile([P, HALF], F32, name="mx", tag="mx", bufs=LAG + 2)
            mn = ring.tile([P, HALF], F32, name="mn", tag="mn")
            gap = ring.tile([P, HALF], F32, name="gap", tag="gap", bufs=LAG + 2)
            th = ring.tile([P, HALF], F32, name="th", tag="th", bufs=LAG + 2)
            nc.vector.tensor_tensor(lo[:].rearrange("p e j -> p j e"), four[:, :, 0:2], four[:, :, 2:4], ALU.min)
            nc.vector.tensor_tensor(hi[:].rearrange("p e j -> p j e"), four[:, :, 0:2], four[:, :, 2:4], ALU.max)
            nc.vector.tensor_tensor(mn[:], lo[:, 0, :], lo[:, 1, :], ALU.min)
            nc.vector.tensor_tensor(mx[:], hi[:, 0, :], hi[:, 1, :], ALU.max)
            nc.vector.tensor_tensor(gap[:], h2[m][:, c : c + HALF], mn[:], ALU.subtract)
            nc.scalar.activation(th[:], gap[:], ACT.Tanh)
            waiting.append((m, c, mx, th))
            if k >= LAG:
                finish(*waiting[k - LAG], hi[:, 0, :])
        for i, unit in enumerate(waiting[-LAG:]):
            last = keep.tile([P, HALF], F32, name=f"last{i}")
            finish(*unit, last[:])
